import numpy as np
import ml_dtypes


def mxq(x, axis, fmt="e4m3"):
    dtype, down = {"e4m3": (ml_dtypes.float8_e4m3fn, 7), "e5m2": (ml_dtypes.float8_e5m2, 14)}[fmt]
    v = np.moveaxis(np.asarray(x, np.float32).astype(ml_dtypes.bfloat16).astype(np.float64), axis, -1)
    blocks = v.reshape(v.shape[:-1] + (-1, 32))
    amax = np.abs(blocks).max(-1, keepdims=True)
    byte = np.maximum(np.where(amax > 0, np.frexp(amax)[1] - 1 + 127, 0) - down, 1)
    scale = np.exp2(byte - 127.0)
    codes = (blocks / scale).astype(np.float32).astype(dtype).astype(np.float64)
    return np.moveaxis((codes * scale).reshape(v.shape), -1, axis)


WIDE = False


def mx_kscale(k):
    if not WIDE:
        return np.ones(k)
    levels = np.array([10, -10, 5, -5, 0])
    if k % 512:
        return np.exp2(np.random.permutation(np.resize(levels, k // 32))).repeat(32)
    a = np.empty((k // 512, 16))
    for p in range(k // 512):
        a[p, :8] = np.random.permutation(np.resize(levels, 8))
        for g in range(8):
            far = levels[np.abs(levels - a[p, g]) >= 10]
            a[p, g + 8] = far[np.random.randint(len(far))]
    return np.exp2(a.ravel()).repeat(32)


def f64(x):
    return np.asarray(x).astype(np.float64)


def striped(idx):
    return np.tile(np.asarray(idx).reshape(-1, 16).T, (8, 1)).astype(np.uint16)


def unstriped(offs):
    return offs[:16].T.reshape(-1).astype(np.int64)


E2M1 = np.array([0.0, 0.5, 1.0, 1.5, 2.0, 3.0, 4.0, 6.0, -0.0, -0.5, -1.0, -1.5, -2.0, -3.0, -4.0, -6.0])


def pack_weight(w, fmt):
    k, n = w.shape
    w = f64(np.asarray(w, np.float32).astype(ml_dtypes.bfloat16)).reshape(k // 32, 32, n)
    amax = np.abs(w).max(1)
    if fmt == "e4m3":
        byte = np.frexp(amax)[1] - 1 + 127 - 7
    else:
        mant, ex = np.frexp(amax / 6.0)
        byte = np.where(mant > 0.5, ex, ex - 1) + 127
    byte = np.clip(np.where(amax > 0, byte, 1), 1, 254)
    scaled = (w * np.exp2(127.0 - byte)[:, None, :]).reshape(k, n).astype(np.float32)
    by_word = np.ascontiguousarray(scaled.reshape(k // 512, 128, 4, n).transpose(0, 1, 3, 2))
    if fmt == "e4m3":
        words = by_word.astype(ml_dtypes.float8_e4m3fn).view(np.uint8)
    else:
        c = by_word.astype(ml_dtypes.float4_e2m1fn).view(np.uint8) & 0xF
        words = (c[..., 0::2] | (c[..., 1::2] << 4)).reshape(k // 512, 128, 2 * n)
    return np.ascontiguousarray(words), np.ascontiguousarray(byte.astype(np.uint8).reshape(k // 512, 16, n))


def unpack_weight(words, scales, fmt):
    g, _, n = scales.shape
    words = np.ascontiguousarray(words).reshape(g, 128, n, -1)
    if fmt == "e4m3":
        vals = words.view(ml_dtypes.float8_e4m3fn).astype(np.float64)
    else:
        nib = np.empty((g, 128, n, 4), np.uint8)
        nib[..., 0::2] = words & 0xF
        nib[..., 1::2] = words >> 4
        vals = E2M1[nib]
    vals = vals * np.repeat(np.exp2(scales.astype(np.float64) - 127.0), 8, axis=1)[..., None]
    return vals.transpose(0, 1, 3, 2).reshape(g * 512, n)


D, E, T, I, Q = 512, 512, 2048, 512, 128


def setup_inputs():
    n = np.random.standard_normal
    idx2 = np.random.permutation(I)[:I]
    idx = np.random.permutation(T)[:I]
    fd = mx_kscale(D)
    fi = mx_kscale(I)
    ti = np.ones(T)
    ti[idx] = fi
    keysp = pack_weight(n((D, T)) / fd[:, None], "e2m1")
    return {
        "query": (n((D, Q)) * 0.7 / np.sqrt(D) * fd[:, None]).astype(np.float32),
        "keys_words": keysp[0],
        "keys_scales": keysp[1],
        "os": (np.random.uniform(4.0, 16.0, (1, I)) * fi).astype(np.float32),
        "vals": (n((E, T)) / ti).astype(np.float32),
        "offs2": striped(idx2),
        "offs": striped(idx),
    }


def reference(query, keys_words, keys_scales, os, vals, offs2, offs):
    idx2 = unstriped(offs2)
    idx = unstriped(offs)
    keysu = unpack_weight(keys_words, keys_scales, "e2m1")
    queryq = mxq(f64(query), 0, "e4m3")
    keysidxg = keysu[:, idx]
    a = queryq.T @ keysidxg
    pa = np.exp(a)
    pb = np.sqrt(pa)
    p = pa * pb[:, idx2]
    z = np.sum(p, axis=1, keepdims=True)
    w = p / z
    wo1 = w * f64(os)
    wt1 = wo1.T
    vt1 = f64(vals)[:, idx].T
    wt1q = mxq(wt1, 0, "e4m3")
    vt1q = mxq(vt1, 0, "e4m3")
    o = wt1q.T @ vt1q
    return o

@@ -1,0 +1,158 @@
+from contextlib import ExitStack
+
+import concourse.mybir as mybir
+from concourse.masks import make_identity
+
+D, E, T, I, Q = 512, 512, 2048, 512, 128
+FLOPS = 2 * Q * D * I + 2 * Q * I * E
+
+F32 = mybir.dt.float32
+BF16 = mybir.dt.bfloat16
+I32 = mybir.dt.int32
+U32 = mybir.dt.uint32
+U16 = mybir.dt.uint16
+U8 = mybir.dt.uint8
+FP8X4 = mybir.dt.float8_e4m3fn_x4
+FP4X4 = mybir.dt.float4_e2m1fn_x4
+ACT = mybir.ActivationFunctionType
+ALU = mybir.AluOpType
+
+P = 128
+PACK = 4
+LINK_WINDOW = 704
+
+
+def tile_attend_linkedproduct_kernel(tc, query, keys_words, keys_scales, slot_factor, vals, offs2, offs, out):
+    nc = tc.nc
+    with ExitStack() as ctx:
+        sb = ctx.enter_context(tc.tile_pool(name="sb", bufs=1))
+        ps = ctx.enter_context(tc.psum_pool(name="ps", bufs=1))
+        ps_turn = ctx.enter_context(tc.psum_pool(name="ps_turn", bufs=3))
+        ps_out = ctx.enter_context(tc.psum_pool(name="ps_out", bufs=2))
+
+        idx = sb.tile([P, I // 16], U16, name="idx")
+        idx2 = sb.tile([P, I // 16], U16, name="idx2")
+        pool_words = sb.tile([P, T], U16, name="pool_words", align_bytes=64)
+        pool_scales = sb.tile([P, T], U8, name="pool_scales", align_bytes=64)
+        q_raw = sb.tile([P, PACK, Q], F32, name="q_raw")
+        os_col = sb.tile([P, PACK], F32, name="os_col")
+        pool_vals = [sb.tile([P, T], F32, name=f"pool_vals{j}", align_bytes=64) for j in range(E // P)]
+        ident = sb.tile([P, P], F32, name="ident")
+        pb = sb.tile([P, LINK_WINDOW], F32, name="pb", align_bytes=64)
+
+        nc.vector.memset(pool_scales[:].bitcast(I32), 0)
+        nc.vector.memset(pb[:, I:], 0.0)
+        nc.scalar.activation(out=pb[:, I:], in_=pb[:, I:], func=ACT.Exp)
+        make_identity(nc, ident[:])
+
+        nc.sync.dma_start(idx[:], offs)
+        nc.sync.dma_start(out=pool_words[:].bitcast(I32), in_=keys_words[0].bitcast(I32))
+        for quad in range(4):
+            nc.sync.dma_start(
+                out=pool_scales[32 * quad : 32 * quad + 4, :].bitcast(I32),
+                in_=keys_scales[0, 4 * quad : 4 * quad + 4, :].bitcast(I32),
+            )
+        nc.sync.dma_start(out=q_raw[:], in_=query.rearrange("(p t) q -> p t q", t=PACK))
+        nc.sync.dma_start(out=pool_vals[0][:], in_=vals[0:P, :])
+        nc.sync.dma_start(out=os_col[:], in_=slot_factor.rearrange("o (p t) -> p (o t)", t=PACK))
+        nc.sync.dma_start(idx2[:], offs2)
+        for j in range(1, E // P):
+            nc.sync.dma_start(out=pool_vals[j][:], in_=vals[j * P : (j + 1) * P, :])
+
+        def quantise(grouped, name):
+            codes = sb.tile([P, P], U32, name=name + "_codes", align_bytes=64)
+            scales = sb.tile([P, P], U8, name=name + "_scales", align_bytes=64)
+            nc.vector.quantize_mx(out=codes[:].bitcast(FP8X4), scales=scales[:], in_=grouped[:])
+            return codes, scales
+
+        def turn(rows, name):
+            words = rows[:].bitcast(F32)
+            turned = ps_turn.tile([P, 2, P], F32, name="turned")
+            for u in range(2):
+                nc.tensor.transpose(turned[:, u, :], words[:, u : I // 2 : 2], ident[:])
+            grouped = sb.tile([P, P * PACK], BF16, name=name + "_grouped", align_bytes=64)
+            nc.scalar.copy(
+                out=grouped[:].bitcast(F32).rearrange("p (c u) -> p c u", u=2),
+                in_=turned[:].rearrange("p u c -> p c u"),
+            )
+            return grouped
+
+        def gather_vals(j):
+            picked = sb.tile([P, I], BF16, name=f"picked{j}", align_bytes=64)
+            nc.vector.tensor_copy(picked[:], pool_vals[j][:].indirect(idx[:]))
+            return picked
+
+        key_words = sb.tile([P, I], U16, name="key_words", align_bytes=64)
+        key_scales = sb.tile([P, I], U8, name="key_scales", align_bytes=64)
+        nc.vector.tensor_copy(key_words[:], pool_words[:].indirect(idx[:]))
+        nc.vector.tensor_copy(key_scales[:], pool_scales[:].indirect(idx[:]))
+
+        q_grouped = sb.tile([P, Q * PACK], BF16, name="q_grouped", align_bytes=64)
+        nc.scalar.copy(
+            out=q_grouped[:].rearrange("p (q t) -> p q t", t=PACK),
+            in_=q_raw[:].rearrange("p t q -> p q t"),
+        )
+        q_codes, q_scales = quantise(q_grouped, "q")
+
+        a = ps.tile([P, I], F32, name="a")
+        nc.tensor.matmul_mx(
+            out=a[:], lhsT=q_codes[:].bitcast(FP8X4), lhsT_scale=q_scales[:],
+            rhs=key_words[:].bitcast(FP4X4), rhs_scale=key_scales[:], start=True, stop=True,
+        )
+
+        os_rows = ps.tile([P, PACK, P], F32, name="os_rows")
+        for t in range(PACK):
+            nc.tensor.transpose(os_rows[:, t, :], os_col[:, t : t + 1].to_broadcast([P, P]), ident[:])
+
+        neg_half_a = sb.tile([P, I], F32, name="neg_half_a")
+        neg_half_max = sb.tile([P, 1], F32, name="neg_half_max")
+        nc.vector.tensor_scalar(
+            out=neg_half_a[:], in0=a[:], scalar1=-0.5, scalar2=None, op0=ALU.mult, op1=ALU.min,
+            accum_out=neg_half_max[:],
+        )
+        nc.scalar.activation(out=pb[:, :I], in_=neg_half_a[:], func=ACT.Exp, scale=-1.0, bias=neg_half_max[:])
+        pa = sb.tile([P, I], F32, name="pa")
+        nc.scalar.activation(out=pa[:], in_=pb[:, :I], func=ACT.Square)
+
+        picked = gather_vals(0)
+        v_grouped = [turn(picked, "v0")]
+
+        pb_linked = sb.tile([P, I], F32, name="pb_linked")
+        nc.vector.tensor_copy(pb_linked[:], pb[:].indirect(idx2[:]))
+        v_mx = [quantise(v_grouped[0], "v0")]
+        p = sb.tile([P, I], F32, name="p")
+        z = sb.tile([P, 1], F32, name="z")
+        nc.vector.scalar_tensor_tensor(
+            out=p[:], in0=pb_linked[:], scalar=1.0, in1=pa[:], op0=ALU.mult, op1=ALU.mult, accum_out=z[:]
+        )
+        inv_z = sb.tile([P, 1], F32, name="inv_z")
+        nc.vector.reciprocal(out=inv_z[:], in_=z[:])
+        wo = sb.tile([P, I], BF16, name="wo", align_bytes=64)
+        nc.vector.scalar_tensor_tensor(
+            out=wo[:].rearrange("q (s t) -> q s t", t=PACK),
+            in0=p[:].rearrange("q (s t) -> q s t", t=PACK),
+            scalar=inv_z[:],
+            in1=os_rows[:].rearrange("q t s -> q s t"),
+            op0=ALU.mult, op1=ALU.mult,
+        )
+        w_grouped = turn(wo, "w")
+
+        def product(j):
+            acc = ps_out.tile([P, P], F32, name="acc")
+            nc.tensor.matmul_mx(
+                out=acc[:], lhsT=w_codes[:].bitcast(FP8X4), lhsT_scale=w_scales[:],
+                rhs=v_mx[j][0][:].bitcast(FP8X4), rhs_scale=v_mx[j][1][:], start=True, stop=True,
+            )
+            res = sb.tile([P, P], F32, name=f"res{j}")
+            nc.scalar.copy(out=res[:], in_=acc[:])
+            nc.sync.dma_start(out=out[:, j * P : (j + 1) * P], in_=res[:])
+
+        v_grouped.append(turn(gather_vals(1), "v1"))
+        w_codes, w_scales = quantise(w_grouped, "w")
+        product(0)
+        for j in range(2, E // P):
+            v_grouped.append(turn(gather_vals(j), f"v{j}"))
+            v_mx.append(quantise(v_grouped[j - 1], f"v{j - 1}"))
+            product(j - 1)
+        v_mx.append(quantise(v_grouped[3], "v3"))
+        product(3)

@@ -27,8 +27,7 @@ def tile_attend_linkedproduct_kernel(tc, query, keys_words, keys_scales, slot_fa
     with ExitStack() as ctx:
         sb = ctx.enter_context(tc.tile_pool(name="sb", bufs=1))
         ps = ctx.enter_context(tc.psum_pool(name="ps", bufs=1))
-        ps_turn = ctx.enter_context(tc.psum_pool(name="ps_turn", bufs=3))
-        ps_out = ctx.enter_context(tc.psum_pool(name="ps_out", bufs=2))
+        ps_turn = ctx.enter_context(tc.psum_pool(name="ps_turn", bufs=5))
 
         idx = sb.tile([P, I // 16], U16, name="idx")
         idx2 = sb.tile([P, I // 16], U16, name="idx2")
@@ -36,46 +35,44 @@ def tile_attend_linkedproduct_kernel(tc, query, keys_words, keys_scales, slot_fa
         pool_scales = sb.tile([P, T], U8, name="pool_scales", align_bytes=64)
         q_raw = sb.tile([P, PACK, Q], F32, name="q_raw")
         os_col = sb.tile([P, PACK], F32, name="os_col")
-        pool_vals = [sb.tile([P, T], F32, name=f"pool_vals{j}", align_bytes=64) for j in range(E // P)]
+        pool_vals = {j: sb.tile([P, T], F32, name=f"pool_vals{j}", tag=f"slot{j}", align_bytes=64) for j in (0, 1, 3)}
+        raw_halves = [sb.tile([P, T // 2], F32, name=f"raw_half{h}", align_bytes=64) for h in range(2)]
         ident = sb.tile([P, P], F32, name="ident")
         pb = sb.tile([P, LINK_WINDOW], F32, name="pb", align_bytes=64)
 
         nc.vector.memset(pool_scales[:].bitcast(I32), 0)
-        nc.vector.memset(pb[:, I:], 0.0)
+        nc.gpsimd.memset(pb[:, I:], 0.0)
         nc.scalar.activation(out=pb[:, I:], in_=pb[:, I:], func=ACT.Exp)
         make_identity(nc, ident[:])
 
-        nc.sync.dma_start(idx[:], offs)
         nc.sync.dma_start(out=pool_words[:].bitcast(I32), in_=keys_words[0].bitcast(I32))
-        for quad in range(4):
-            nc.sync.dma_start(
-                out=pool_scales[32 * quad : 32 * quad + 4, :].bitcast(I32),
-                in_=keys_scales[0, 4 * quad : 4 * quad + 4, :].bitcast(I32),
-            )
+        nc.sync.dma_start(idx[:], offs)
         nc.sync.dma_start(out=q_raw[:], in_=query.rearrange("(p t) q -> p t q", t=PACK))
+        for r in range(4):
+            nc.sync.dma_start(
+                out=pool_scales[r:P:32, :].bitcast(I32),
+                in_=keys_scales[0, r:16:4, :].bitcast(I32),
+            )
+        nc.sync.dma_start(out=raw_halves[0][:], in_=vals[2 * P : 3 * P, : T // 2])
         nc.sync.dma_start(out=pool_vals[0][:], in_=vals[0:P, :])
         nc.sync.dma_start(out=os_col[:], in_=slot_factor.rearrange("o (p t) -> p (o t)", t=PACK))
         nc.sync.dma_start(idx2[:], offs2)
-        for j in range(1, E // P):
-            nc.sync.dma_start(out=pool_vals[j][:], in_=vals[j * P : (j + 1) * P, :])
+        nc.sync.dma_start(out=pool_vals[1][:], in_=vals[P : 2 * P, :])
+        nc.sync.dma_start(out=raw_halves[1][:], in_=vals[2 * P : 3 * P, T // 2 :])
+        nc.sync.dma_start(out=pool_vals[3][:], in_=vals[3 * P :, :])
 
-        def quantise(grouped, name):
-            codes = sb.tile([P, P], U32, name=name + "_codes", align_bytes=64)
-            scales = sb.tile([P, P], U8, name=name + "_scales", align_bytes=64)
-            nc.vector.quantize_mx(out=codes[:].bitcast(FP8X4), scales=scales[:], in_=grouped[:])
-            return codes, scales
+        def quantise(codes, scales, grouped):
+            nc.vector.quantize_mx(out=codes.bitcast(FP8X4), scales=scales, in_=grouped)
 
-        def turn(rows, name):
+        def turn(rows, grouped):
             words = rows[:].bitcast(F32)
             turned = ps_turn.tile([P, 2, P], F32, name="turned")
             for u in range(2):
                 nc.tensor.transpose(turned[:, u, :], words[:, u : I // 2 : 2], ident[:])
-            grouped = sb.tile([P, P * PACK], BF16, name=name + "_grouped", align_bytes=64)
             nc.scalar.copy(
-                out=grouped[:].bitcast(F32).rearrange("p (c u) -> p c u", u=2),
+                out=grouped.bitcast(F32).rearrange("p (c u) -> p c u", u=2),
                 in_=turned[:].rearrange("p u c -> p c u"),
             )
-            return grouped
 
         def gather_vals(j):
             picked = sb.tile([P, I], BF16, name=f"picked{j}", align_bytes=64)
@@ -83,76 +80,103 @@ def tile_attend_linkedproduct_kernel(tc, query, keys_words, keys_scales, slot_fa
             return picked
 
         key_words = sb.tile([P, I], U16, name="key_words", align_bytes=64)
-        key_scales = sb.tile([P, I], U8, name="key_scales", align_bytes=64)
         nc.vector.tensor_copy(key_words[:], pool_words[:].indirect(idx[:]))
-        nc.vector.tensor_copy(key_scales[:], pool_scales[:].indirect(idx[:]))
 
-        q_grouped = sb.tile([P, Q * PACK], BF16, name="q_grouped", align_bytes=64)
+        q_grouped = sb.tile([P, Q * PACK], BF16, name="q_grouped", tag="slot_keys1", align_bytes=64)
         nc.scalar.copy(
             out=q_grouped[:].rearrange("p (q t) -> p q t", t=PACK),
             in_=q_raw[:].rearrange("p t q -> p q t"),
         )
-        q_codes, q_scales = quantise(q_grouped, "q")
+        q_codes = sb.tile([P, Q], U32, name="q_codes", align_bytes=64)
+        q_scales = sb.tile([P, Q], U8, name="q_scales", align_bytes=64)
+        quantise(q_codes[:], q_scales[:], q_grouped[:])
 
-        a = ps.tile([P, I], F32, name="a")
-        nc.tensor.matmul_mx(
-            out=a[:], lhsT=q_codes[:].bitcast(FP8X4), lhsT_scale=q_scales[:],
-            rhs=key_words[:].bitcast(FP4X4), rhs_scale=key_scales[:], start=True, stop=True,
-        )
+        pool_vals2_bf16 = sb.tile([P, T], BF16, name="pool_vals2_bf16", tag="slot_bf16", align_bytes=64)
+        nc.scalar.activation(out=pool_vals2_bf16[:, : T // 2], in_=raw_halves[0][:], func=ACT.Copy)
 
-        os_rows = ps.tile([P, PACK, P], F32, name="os_rows")
+        half = I // 2
+        a = []
+        for h in range(2):
+            key_scales = sb.tile([P, half], U8, name=f"key_scales{h}", tag=f"slot_keys{h}", align_bytes=64)
+            nc.vector.tensor_copy(key_scales[:], pool_scales[:].indirect(idx[:, h * half // 16 : (h + 1) * half // 16]))
+            a.append(ps.tile([P, half], F32, name=f"a{h}", tag=f"a{h}"))
+            nc.tensor.matmul_mx(
+                out=a[h][:], lhsT=q_codes[:].bitcast(FP8X4), lhsT_scale=q_scales[:],
+                rhs=key_words[:, h * half : (h + 1) * half].bitcast(FP4X4), rhs_scale=key_scales[:],
+                start=True, stop=True,
+            )
+
+        neg_half_a = sb.tile([P, I], F32, name="neg_half_a")
+        running = None
+        for h in range(2):
+            neg_half_max = sb.tile([P, 1], F32, name=f"neg_half_max{h}")
+            nc.vector.tensor_scalar(
+                out=neg_half_a[:, h * half : (h + 1) * half], in0=a[h][:], scalar1=-0.5, scalar2=running,
+                op0=ALU.mult, op1=ALU.min, accum_out=neg_half_max[:],
+            )
+            running = neg_half_max[:]
+        neg_max = sb.tile([P, 1], F32, name="neg_max")
+        nc.scalar.activation(out=neg_max[:], in_=running, func=ACT.Copy, scale=2.0)
+        nc.scalar.activation(out=pb[:, :I], in_=neg_half_a[:], func=ACT.Exp, scale=-1.0, bias=running)
+        pa = sb.tile([P, I], F32, name="pa")
+        nc.scalar.activation(out=pa[:], in_=neg_half_a[:], func=ACT.Exp, scale=-2.0, bias=neg_max[:])
+
+        os_rows = ps.tile([P, PACK, P], F32, name="os_rows", tag="os_rows")
         for t in range(PACK):
             nc.tensor.transpose(os_rows[:, t, :], os_col[:, t : t + 1].to_broadcast([P, P]), ident[:])
 
-        neg_half_a = sb.tile([P, I], F32, name="neg_half_a")
-        neg_half_max = sb.tile([P, 1], F32, name="neg_half_max")
-        nc.vector.tensor_scalar(
-            out=neg_half_a[:], in0=a[:], scalar1=-0.5, scalar2=None, op0=ALU.mult, op1=ALU.min,
-            accum_out=neg_half_max[:],
-        )
-        nc.scalar.activation(out=pb[:, :I], in_=neg_half_a[:], func=ACT.Exp, scale=-1.0, bias=neg_half_max[:])
-        pa = sb.tile([P, I], F32, name="pa")
-        nc.scalar.activation(out=pa[:], in_=pb[:, :I], func=ACT.Square)
+        v_last = sb.tile([P, I], BF16, name="v_last", tag="slot_res0", align_bytes=64)
+        last_codes = sb.tile([P, P], U32, name="last_codes", align_bytes=64)
+        last_scales = sb.tile([P, P], U8, name="last_scales", align_bytes=64)
 
-        picked = gather_vals(0)
-        v_grouped = [turn(picked, "v0")]
+        v_first = sb.tile([P, I], BF16, name="v_first", align_bytes=64)
+        turn(gather_vals(0), v_first[:])
+        p = sb.tile([P, I], F32, name="p", tag="slot0", align_bytes=64)
+        nc.vector.tensor_tensor(p[:], pb[:].indirect(idx2[:]), pa[:], ALU.mult)
 
-        pb_linked = sb.tile([P, I], F32, name="pb_linked")
-        nc.vector.tensor_copy(pb_linked[:], pb[:].indirect(idx2[:]))
-        v_mx = [quantise(v_grouped[0], "v0")]
-        p = sb.tile([P, I], F32, name="p")
+        nc.scalar.activation(out=pool_vals2_bf16[:, T // 2 :], in_=raw_halves[1][:], func=ACT.Copy)
+        p_summed = sb.tile([P, I], F32, name="p_summed")
         z = sb.tile([P, 1], F32, name="z")
-        nc.vector.scalar_tensor_tensor(
-            out=p[:], in0=pb_linked[:], scalar=1.0, in1=pa[:], op0=ALU.mult, op1=ALU.mult, accum_out=z[:]
-        )
-        inv_z = sb.tile([P, 1], F32, name="inv_z")
+        nc.scalar.activation(out=p_summed[:], in_=p[:], func=ACT.Copy, accum_out=z[:])
+        picked2 = sb.tile([P, I], BF16, name="picked2", align_bytes=64)
+        nc.scalar.activation(out=picked2[:], in_=pool_vals2_bf16[:].indirect(idx[:]), func=ACT.Copy)
+
+        picked1 = gather_vals(1)
+        inv_z = sb.tile([P, 1], F32, name="inv_z", tag="slot1", align_bytes=64)
         nc.vector.reciprocal(out=inv_z[:], in_=z[:])
         wo = sb.tile([P, I], BF16, name="wo", align_bytes=64)
         nc.vector.scalar_tensor_tensor(
             out=wo[:].rearrange("q (s t) -> q s t", t=PACK),
-            in0=p[:].rearrange("q (s t) -> q s t", t=PACK),
+            in0=p_summed[:].rearrange("q (s t) -> q s t", t=PACK),
             scalar=inv_z[:],
             in1=os_rows[:].rearrange("q t s -> q s t"),
             op0=ALU.mult, op1=ALU.mult,
         )
-        w_grouped = turn(wo, "w")
+        early = sb.tile([P, 3 * I], BF16, name="early", tag="slot_bf16", align_bytes=64)
+        turn(picked1, early[:, :I])
+        turn(wo, early[:, 2 * I :])
+        turn(picked2, early[:, I : 2 * I])
 
-        def product(j):
-            acc = ps_out.tile([P, P], F32, name="acc")
+        picked3 = gather_vals(3)
+        turn(picked3, v_last[:])
+        early_codes = sb.tile([P, 4 * P], U32, name="early_codes", tag="slot3", align_bytes=64)
+        early_scales = sb.tile([P, 4 * P], U8, name="early_scales", align_bytes=64)
+        for place, grouped in ((0, v_first[:]), (1, early[:, :I]), (3, early[:, 2 * I :]), (2, early[:, I : 2 * I])):
+            cols = slice(place * P, (place + 1) * P)
+            quantise(early_codes[:, cols], early_scales[:, cols], grouped)
+        quantise(last_codes[:], last_scales[:], v_last[:])
+
+        def product(first, last, codes, scales, bank, copy_out):
+            width = (last - first) * P
+            acc = ps.tile([P, width], F32, name=f"acc{first}", tag=bank)
             nc.tensor.matmul_mx(
-                out=acc[:], lhsT=w_codes[:].bitcast(FP8X4), lhsT_scale=w_scales[:],
-                rhs=v_mx[j][0][:].bitcast(FP8X4), rhs_scale=v_mx[j][1][:], start=True, stop=True,
+                out=acc[:], lhsT=early_codes[:, 3 * P :].bitcast(FP8X4), lhsT_scale=early_scales[:, 3 * P :],
+                rhs=codes.bitcast(FP8X4), rhs_scale=scales, start=True, stop=True,
             )
-            res = sb.tile([P, P], F32, name=f"res{j}")
-            nc.scalar.copy(out=res[:], in_=acc[:])
-            nc.sync.dma_start(out=out[:, j * P : (j + 1) * P], in_=res[:])
+            res = sb.tile([P, width], F32, name=f"res{first}", tag=f"slot_res{first}", align_bytes=64)
+            copy_out(out=res[:], in_=acc[:])
+            nc.sync.dma_start(out=out[:, first * P : last * P], in_=res[:])
 
-        v_grouped.append(turn(gather_vals(1), "v1"))
-        w_codes, w_scales = quantise(w_grouped, "w")
-        product(0)
-        for j in range(2, E // P):
-            v_grouped.append(turn(gather_vals(j), f"v{j}"))
-            v_mx.append(quantise(v_grouped[j - 1], f"v{j - 1}"))
-            product(j - 1)
-        v_mx.append(quantise(v_grouped[3], "v3"))
-        product(3)
+        product(0, 2, early_codes[:, : 2 * P], early_scales[:, : 2 * P], "a0", nc.vector.tensor_copy)
+        product(2, 3, early_codes[:, 2 * P : 3 * P], early_scales[:, 2 * P : 3 * P], "os_rows", nc.scalar.copy)
+        product(3, 4, last_codes[:], last_scales[:], "a1", nc.scalar.copy)

@@ -19,7 +19,11 @@ ALU = mybir.AluOpType
 
 P = 128
 PACK = 4
-LINK_WINDOW = 704
+LIST_ROWS = 16
+HALF = I // 2
+LINK_COLUMNS = 704
+EARLY_TOKENS = 5 * T // 8
+TURN_BANKS = 5
 
 
 def tile_attend_linkedproduct_kernel(tc, query, keys_words, keys_scales, slot_factor, vals, offs2, offs, out):
@@ -27,42 +31,42 @@ def tile_attend_linkedproduct_kernel(tc, query, keys_words, keys_scales, slot_fa
     with ExitStack() as ctx:
         sb = ctx.enter_context(tc.tile_pool(name="sb", bufs=1))
         ps = ctx.enter_context(tc.psum_pool(name="ps", bufs=1))
-        ps_turn = ctx.enter_context(tc.psum_pool(name="ps_turn", bufs=5))
+        ps_turn = ctx.enter_context(tc.psum_pool(name="ps_turn", bufs=TURN_BANKS))
 
-        idx = sb.tile([P, I // 16], U16, name="idx")
-        idx2 = sb.tile([P, I // 16], U16, name="idx2")
+        idx = sb.tile([P, I // LIST_ROWS], U16, name="idx")
+        idx2 = sb.tile([P, I // LIST_ROWS], U16, name="idx2")
         pool_words = sb.tile([P, T], U16, name="pool_words", align_bytes=64)
         pool_scales = sb.tile([P, T], U8, name="pool_scales", align_bytes=64)
         q_raw = sb.tile([P, PACK, Q], F32, name="q_raw")
-        os_col = sb.tile([P, PACK], F32, name="os_col")
-        pool_vals = {j: sb.tile([P, T], F32, name=f"pool_vals{j}", tag=f"slot{j}", align_bytes=64) for j in (0, 1, 3)}
-        raw_halves = [sb.tile([P, T // 2], F32, name=f"raw_half{h}", align_bytes=64) for h in range(2)]
+        factor_columns = sb.tile([P, PACK], F32, name="factor_columns")
+        pool_vals = {j: sb.tile([P, T], F32, name=f"pool_vals{j}", tag=f"vals{j}", align_bytes=64) for j in (0, 1, 3)}
+        block2_early = sb.tile([P, EARLY_TOKENS], F32, name="block2_early", tag="running1", align_bytes=64)
+        block2_late = sb.tile([P, T - EARLY_TOKENS], F32, name="block2_late", align_bytes=64)
         ident = sb.tile([P, P], F32, name="ident")
-        pb = sb.tile([P, LINK_WINDOW], F32, name="pb", align_bytes=64)
+        pb = sb.tile([P, LINK_COLUMNS], F32, name="pb", align_bytes=64)
 
         nc.vector.memset(pool_scales[:].bitcast(I32), 0)
         nc.gpsimd.memset(pb[:, I:], 0.0)
-        nc.scalar.activation(out=pb[:, I:], in_=pb[:, I:], func=ACT.Exp)
         make_identity(nc, ident[:])
 
         nc.sync.dma_start(out=pool_words[:].bitcast(I32), in_=keys_words[0].bitcast(I32))
         nc.sync.dma_start(idx[:], offs)
-        nc.sync.dma_start(out=q_raw[:], in_=query.rearrange("(p t) q -> p t q", t=PACK))
+        nc.sync.dma_start(out=q_raw[:], in_=query.rearrange("(s t) q -> s t q", t=PACK))
         for r in range(4):
             nc.sync.dma_start(
                 out=pool_scales[r:P:32, :].bitcast(I32),
                 in_=keys_scales[0, r:16:4, :].bitcast(I32),
             )
-        nc.sync.dma_start(out=raw_halves[0][:], in_=vals[2 * P : 3 * P, : T // 2])
+        nc.sync.dma_start(out=block2_early[:], in_=vals[2 * P : 3 * P, :EARLY_TOKENS])
         nc.sync.dma_start(out=pool_vals[0][:], in_=vals[0:P, :])
-        nc.sync.dma_start(out=os_col[:], in_=slot_factor.rearrange("o (p t) -> p (o t)", t=PACK))
+        nc.sync.dma_start(out=factor_columns[:], in_=slot_factor.rearrange("o (s t) -> s (o t)", t=PACK))
         nc.sync.dma_start(idx2[:], offs2)
         nc.sync.dma_start(out=pool_vals[1][:], in_=vals[P : 2 * P, :])
-        nc.sync.dma_start(out=raw_halves[1][:], in_=vals[2 * P : 3 * P, T // 2 :])
+        nc.sync.dma_start(out=block2_late[:], in_=vals[2 * P : 3 * P, EARLY_TOKENS:])
         nc.sync.dma_start(out=pool_vals[3][:], in_=vals[3 * P :, :])
 
-        def quantise(codes, scales, grouped):
-            nc.vector.quantize_mx(out=codes.bitcast(FP8X4), scales=scales, in_=grouped)
+        def quantise(to_codes, to_scales, grouped):
+            nc.vector.quantize_mx(out=to_codes.bitcast(FP8X4), scales=to_scales, in_=grouped)
 
         def turn(rows, grouped):
             words = rows[:].bitcast(F32)
@@ -70,8 +74,8 @@ def tile_attend_linkedproduct_kernel(tc, query, keys_words, keys_scales, slot_fa
             for u in range(2):
                 nc.tensor.transpose(turned[:, u, :], words[:, u : I // 2 : 2], ident[:])
             nc.scalar.copy(
-                out=grouped.bitcast(F32).rearrange("p (c u) -> p c u", u=2),
-                in_=turned[:].rearrange("p u c -> p c u"),
+                out=grouped.bitcast(F32).rearrange("s (c u) -> s c u", u=2),
+                in_=turned[:].rearrange("s u c -> s c u"),
             )
 
         def gather_vals(j):
@@ -82,101 +86,104 @@ def tile_attend_linkedproduct_kernel(tc, query, keys_words, keys_scales, slot_fa
         key_words = sb.tile([P, I], U16, name="key_words", align_bytes=64)
         nc.vector.tensor_copy(key_words[:], pool_words[:].indirect(idx[:]))
 
-        q_grouped = sb.tile([P, Q * PACK], BF16, name="q_grouped", tag="slot_keys1", align_bytes=64)
-        nc.scalar.copy(
-            out=q_grouped[:].rearrange("p (q t) -> p q t", t=PACK),
-            in_=q_raw[:].rearrange("p t q -> p q t"),
+        q_grouped = sb.tile([P, Q * PACK], BF16, name="q_grouped", tag="key_scales1", align_bytes=64)
+        nc.scalar.activation(
+            out=q_grouped[:].rearrange("s (q t) -> s q t", t=PACK),
+            in_=q_raw[:].rearrange("s t q -> s q t"),
+            func=ACT.Copy,
         )
         q_codes = sb.tile([P, Q], U32, name="q_codes", align_bytes=64)
         q_scales = sb.tile([P, Q], U8, name="q_scales", align_bytes=64)
         quantise(q_codes[:], q_scales[:], q_grouped[:])
 
-        pool_vals2_bf16 = sb.tile([P, T], BF16, name="pool_vals2_bf16", tag="slot_bf16", align_bytes=64)
-        nc.scalar.activation(out=pool_vals2_bf16[:, : T // 2], in_=raw_halves[0][:], func=ACT.Copy)
+        block2_bf16 = sb.tile([P, T], BF16, name="block2_bf16", tag="block2_bf16", align_bytes=64)
+        nc.scalar.activation(out=block2_bf16[:, :EARLY_TOKENS], in_=block2_early[:], func=ACT.Copy)
 
-        half = I // 2
-        a = []
+        scores = []
         for h in range(2):
-            key_scales = sb.tile([P, half], U8, name=f"key_scales{h}", tag=f"slot_keys{h}", align_bytes=64)
-            nc.vector.tensor_copy(key_scales[:], pool_scales[:].indirect(idx[:, h * half // 16 : (h + 1) * half // 16]))
-            a.append(ps.tile([P, half], F32, name=f"a{h}", tag=f"a{h}"))
+            key_scales = sb.tile([P, HALF], U8, name=f"key_scales{h}", tag=f"key_scales{h}", align_bytes=64)
+            entries = idx[:, h * HALF // LIST_ROWS : (h + 1) * HALF // LIST_ROWS]
+            nc.vector.tensor_copy(key_scales[:], pool_scales[:].indirect(entries))
+            scores.append(ps.tile([P, HALF], F32, name=f"scores{h}", tag=f"bank{h}"))
             nc.tensor.matmul_mx(
-                out=a[h][:], lhsT=q_codes[:].bitcast(FP8X4), lhsT_scale=q_scales[:],
-                rhs=key_words[:, h * half : (h + 1) * half].bitcast(FP4X4), rhs_scale=key_scales[:],
+                out=scores[h][:], lhsT=q_codes[:].bitcast(FP8X4), lhsT_scale=q_scales[:],
+                rhs=key_words[:, h * HALF : (h + 1) * HALF].bitcast(FP4X4), rhs_scale=key_scales[:],
                 start=True, stop=True,
             )
 
         neg_half_a = sb.tile([P, I], F32, name="neg_half_a")
-        running = None
+        neg_half_max = None
         for h in range(2):
-            neg_half_max = sb.tile([P, 1], F32, name=f"neg_half_max{h}")
+            running = sb.tile([P, 1], F32, name=f"running{h}", tag=f"running{h}", align_bytes=64)
             nc.vector.tensor_scalar(
-                out=neg_half_a[:, h * half : (h + 1) * half], in0=a[h][:], scalar1=-0.5, scalar2=running,
-                op0=ALU.mult, op1=ALU.min, accum_out=neg_half_max[:],
+                out=neg_half_a[:, h * HALF : (h + 1) * HALF], in0=scores[h][:], scalar1=-0.5, scalar2=neg_half_max,
+                op0=ALU.mult, op1=ALU.min, accum_out=running[:],
             )
-            running = neg_half_max[:]
+            neg_half_max = running[:]
         neg_max = sb.tile([P, 1], F32, name="neg_max")
-        nc.scalar.activation(out=neg_max[:], in_=running, func=ACT.Copy, scale=2.0)
-        nc.scalar.activation(out=pb[:, :I], in_=neg_half_a[:], func=ACT.Exp, scale=-1.0, bias=running)
+        nc.scalar.activation(out=neg_max[:], in_=neg_half_max, func=ACT.Copy, scale=2.0)
+        nc.scalar.activation(out=pb[:, :I], in_=neg_half_a[:], func=ACT.Exp, scale=-1.0, bias=neg_half_max)
         pa = sb.tile([P, I], F32, name="pa")
         nc.scalar.activation(out=pa[:], in_=neg_half_a[:], func=ACT.Exp, scale=-2.0, bias=neg_max[:])
 
-        os_rows = ps.tile([P, PACK, P], F32, name="os_rows", tag="os_rows")
+        factor_rows = ps.tile([P, PACK, P], F32, name="factor_rows", tag="bank2")
         for t in range(PACK):
-            nc.tensor.transpose(os_rows[:, t, :], os_col[:, t : t + 1].to_broadcast([P, P]), ident[:])
+            nc.tensor.transpose(factor_rows[:, t, :], factor_columns[:, t : t + 1].to_broadcast([P, P]), ident[:])
 
-        v_last = sb.tile([P, I], BF16, name="v_last", tag="slot_res0", align_bytes=64)
-        last_codes = sb.tile([P, P], U32, name="last_codes", align_bytes=64)
-        last_scales = sb.tile([P, P], U8, name="last_scales", align_bytes=64)
+        v3_grouped = sb.tile([P, I], BF16, name="v3_grouped", tag="result2", align_bytes=64)
+        v3_codes = sb.tile([P, P], U32, name="v3_codes", align_bytes=64)
+        v3_scales = sb.tile([P, P], U8, name="v3_scales", align_bytes=64)
 
-        v_first = sb.tile([P, I], BF16, name="v_first", align_bytes=64)
-        turn(gather_vals(0), v_first[:])
-        p = sb.tile([P, I], F32, name="p", tag="slot0", align_bytes=64)
+        v0_grouped = sb.tile([P, I], BF16, name="v0_grouped", align_bytes=64)
+        turn(gather_vals(0), v0_grouped[:])
+
+        p = sb.tile([P, I], F32, name="p", tag="vals0", align_bytes=64)
         nc.vector.tensor_tensor(p[:], pb[:].indirect(idx2[:]), pa[:], ALU.mult)
 
-        nc.scalar.activation(out=pool_vals2_bf16[:, T // 2 :], in_=raw_halves[1][:], func=ACT.Copy)
         p_summed = sb.tile([P, I], F32, name="p_summed")
         z = sb.tile([P, 1], F32, name="z")
         nc.scalar.activation(out=p_summed[:], in_=p[:], func=ACT.Copy, accum_out=z[:])
+        nc.scalar.activation(out=block2_bf16[:, EARLY_TOKENS:], in_=block2_late[:], func=ACT.Copy)
         picked2 = sb.tile([P, I], BF16, name="picked2", align_bytes=64)
-        nc.scalar.activation(out=picked2[:], in_=pool_vals2_bf16[:].indirect(idx[:]), func=ACT.Copy)
+        nc.scalar.activation(out=picked2[:], in_=block2_bf16[:].indirect(idx[:]), func=ACT.Copy)
 
         picked1 = gather_vals(1)
-        inv_z = sb.tile([P, 1], F32, name="inv_z", tag="slot1", align_bytes=64)
+        inv_z = sb.tile([P, 1], F32, name="inv_z", tag="vals1", align_bytes=64)
         nc.vector.reciprocal(out=inv_z[:], in_=z[:])
         wo = sb.tile([P, I], BF16, name="wo", align_bytes=64)
         nc.vector.scalar_tensor_tensor(
             out=wo[:].rearrange("q (s t) -> q s t", t=PACK),
             in0=p_summed[:].rearrange("q (s t) -> q s t", t=PACK),
             scalar=inv_z[:],
-            in1=os_rows[:].rearrange("q t s -> q s t"),
+            in1=factor_rows[:].rearrange("q t s -> q s t"),
             op0=ALU.mult, op1=ALU.mult,
         )
-        early = sb.tile([P, 3 * I], BF16, name="early", tag="slot_bf16", align_bytes=64)
-        turn(picked1, early[:, :I])
-        turn(wo, early[:, 2 * I :])
-        turn(picked2, early[:, I : 2 * I])
 
-        picked3 = gather_vals(3)
-        turn(picked3, v_last[:])
-        early_codes = sb.tile([P, 4 * P], U32, name="early_codes", tag="slot3", align_bytes=64)
-        early_scales = sb.tile([P, 4 * P], U8, name="early_scales", align_bytes=64)
-        for place, grouped in ((0, v_first[:]), (1, early[:, :I]), (3, early[:, 2 * I :]), (2, early[:, I : 2 * I])):
+        middle_grouped = sb.tile([P, 3 * I], BF16, name="middle_grouped", tag="block2_bf16", align_bytes=64)
+        v1_grouped, v2_grouped, w_grouped = (middle_grouped[:, n * I : (n + 1) * I] for n in range(3))
+        turn(picked1, v1_grouped)
+        turn(wo, w_grouped)
+        turn(picked2, v2_grouped)
+
+        turn(gather_vals(3), v3_grouped[:])
+        codes = sb.tile([P, 4 * P], U32, name="codes", tag="vals3", align_bytes=64)
+        scales = sb.tile([P, 4 * P], U8, name="scales", align_bytes=64)
+        for place, grouped in ((0, v0_grouped[:]), (1, v1_grouped), (3, w_grouped), (2, v2_grouped)):
             cols = slice(place * P, (place + 1) * P)
-            quantise(early_codes[:, cols], early_scales[:, cols], grouped)
-        quantise(last_codes[:], last_scales[:], v_last[:])
+            quantise(codes[:, cols], scales[:, cols], grouped)
+        quantise(v3_codes[:], v3_scales[:], v3_grouped[:])
 
-        def product(first, last, codes, scales, bank, copy_out):
+        def product(first, last, v_codes, v_scales, bank, copy_out, queue):
             width = (last - first) * P
             acc = ps.tile([P, width], F32, name=f"acc{first}", tag=bank)
             nc.tensor.matmul_mx(
-                out=acc[:], lhsT=early_codes[:, 3 * P :].bitcast(FP8X4), lhsT_scale=early_scales[:, 3 * P :],
-                rhs=codes.bitcast(FP8X4), rhs_scale=scales, start=True, stop=True,
+                out=acc[:], lhsT=codes[:, 3 * P :].bitcast(FP8X4), lhsT_scale=scales[:, 3 * P :],
+                rhs=v_codes.bitcast(FP8X4), rhs_scale=v_scales, start=True, stop=True,
             )
-            res = sb.tile([P, width], F32, name=f"res{first}", tag=f"slot_res{first}", align_bytes=64)
-            copy_out(out=res[:], in_=acc[:])
-            nc.sync.dma_start(out=out[:, first * P : last * P], in_=res[:])
+            result = sb.tile([P, width], F32, name=f"result{first}", tag=f"result{first}", align_bytes=64)
+            copy_out(out=result[:], in_=acc[:])
+            queue.dma_start(out=out[:, first * P : last * P], in_=result[:])
 
-        product(0, 2, early_codes[:, : 2 * P], early_scales[:, : 2 * P], "a0", nc.vector.tensor_copy)
-        product(2, 3, early_codes[:, 2 * P : 3 * P], early_scales[:, 2 * P : 3 * P], "os_rows", nc.scalar.copy)
-        product(3, 4, last_codes[:], last_scales[:], "a1", nc.scalar.copy)
+        product(0, 2, codes[:, : 2 * P], scales[:, : 2 * P], "bank0", nc.scalar.copy, nc.sync)
+        product(2, 3, codes[:, 2 * P : 3 * P], scales[:, 2 * P : 3 * P], "bank2", nc.vector.tensor_copy, nc.sync)
+        product(3, 4, v3_codes[:], v3_scales[:], "bank1", nc.scalar.copy, nc.scalar)

from contextlib import ExitStack

import concourse.mybir as mybir
from concourse.masks import make_identity

D, E, T, I, Q = 512, 512, 2048, 512, 128
FLOPS = 2 * Q * D * I + 2 * Q * I * E

F32 = mybir.dt.float32
BF16 = mybir.dt.bfloat16
I32 = mybir.dt.int32
U32 = mybir.dt.uint32
U16 = mybir.dt.uint16
U8 = mybir.dt.uint8
FP8X4 = mybir.dt.float8_e4m3fn_x4
FP4X4 = mybir.dt.float4_e2m1fn_x4
ACT = mybir.ActivationFunctionType
ALU = mybir.AluOpType

P = 128
PACK = 4
LIST_ROWS = 16
HALF = I // 2
LINK_COLUMNS = 704
EARLY_TOKENS = 5 * T // 8
TURN_BANKS = 5


def tile_attend_linkedproduct_kernel(tc, query, keys_words, keys_scales, slot_factor, vals, offs2, offs, out):
    nc = tc.nc
    with ExitStack() as ctx:
        sb = ctx.enter_context(tc.tile_pool(name="sb", bufs=1))
        ps = ctx.enter_context(tc.psum_pool(name="ps", bufs=1))
        ps_turn = ctx.enter_context(tc.psum_pool(name="ps_turn", bufs=TURN_BANKS))

        idx = sb.tile([P, I // LIST_ROWS], U16, name="idx")
        idx2 = sb.tile([P, I // LIST_ROWS], U16, name="idx2")
        pool_words = sb.tile([P, T], U16, name="pool_words", align_bytes=64)
        pool_scales = sb.tile([P, T], U8, name="pool_scales", align_bytes=64)
        q_raw = sb.tile([P, PACK, Q], F32, name="q_raw")
        factor_columns = sb.tile([P, PACK], F32, name="factor_columns")
        pool_vals = {j: sb.tile([P, T], F32, name=f"pool_vals{j}", tag=f"vals{j}", align_bytes=64) for j in (0, 1, 3)}
        block2_early = sb.tile([P, EARLY_TOKENS], F32, name="block2_early", tag="running1", align_bytes=64)
        block2_late = sb.tile([P, T - EARLY_TOKENS], F32, name="block2_late", align_bytes=64)
        ident = sb.tile([P, P], F32, name="ident")
        pb = sb.tile([P, LINK_COLUMNS], F32, name="pb", align_bytes=64)

        nc.vector.memset(pool_scales[:].bitcast(I32), 0)
        nc.gpsimd.memset(pb[:, I:], 0.0)
        make_identity(nc, ident[:])

        nc.sync.dma_start(out=pool_words[:].bitcast(I32), in_=keys_words[0].bitcast(I32))
        nc.sync.dma_start(idx[:], offs)
        nc.sync.dma_start(out=q_raw[:], in_=query.rearrange("(s t) q -> s t q", t=PACK))
        for r in range(4):
            nc.sync.dma_start(
                out=pool_scales[r:P:32, :].bitcast(I32),
                in_=keys_scales[0, r:16:4, :].bitcast(I32),
            )
        nc.sync.dma_start(out=block2_early[:], in_=vals[2 * P : 3 * P, :EARLY_TOKENS])
        nc.sync.dma_start(out=pool_vals[0][:], in_=vals[0:P, :])
        nc.sync.dma_start(out=factor_columns[:], in_=slot_factor.rearrange("o (s t) -> s (o t)", t=PACK))
        nc.sync.dma_start(idx2[:], offs2)
        nc.sync.dma_start(out=pool_vals[1][:], in_=vals[P : 2 * P, :])
        nc.sync.dma_start(out=block2_late[:], in_=vals[2 * P : 3 * P, EARLY_TOKENS:])
        nc.sync.dma_start(out=pool_vals[3][:], in_=vals[3 * P :, :])

        def quantise(to_codes, to_scales, grouped):
            nc.vector.quantize_mx(out=to_codes.bitcast(FP8X4), scales=to_scales, in_=grouped)

        def turn(rows, grouped):
            words = rows[:].bitcast(F32)
            turned = ps_turn.tile([P, 2, P], F32, name="turned")
            for u in range(2):
                nc.tensor.transpose(turned[:, u, :], words[:, u : I // 2 : 2], ident[:])
            nc.scalar.copy(
                out=grouped.bitcast(F32).rearrange("s (c u) -> s c u", u=2),
                in_=turned[:].rearrange("s u c -> s c u"),
            )

        def gather_vals(j):
            picked = sb.tile([P, I], BF16, name=f"picked{j}", align_bytes=64)
            nc.vector.tensor_copy(picked[:], pool_vals[j][:].indirect(idx[:]))
            return picked

        key_words = sb.tile([P, I], U16, name="key_words", align_bytes=64)
        nc.vector.tensor_copy(key_words[:], pool_words[:].indirect(idx[:]))

        q_grouped = sb.tile([P, Q * PACK], BF16, name="q_grouped", tag="key_scales1", align_bytes=64)
        nc.scalar.activation(
            out=q_grouped[:].rearrange("s (q t) -> s q t", t=PACK),
            in_=q_raw[:].rearrange("s t q -> s q t"),
            func=ACT.Copy,
        )
        q_codes = sb.tile([P, Q], U32, name="q_codes", align_bytes=64)
        q_scales = sb.tile([P, Q], U8, name="q_scales", align_bytes=64)
        quantise(q_codes[:], q_scales[:], q_grouped[:])

        block2_bf16 = sb.tile([P, T], BF16, name="block2_bf16", tag="block2_bf16", align_bytes=64)
        nc.scalar.activation(out=block2_bf16[:, :EARLY_TOKENS], in_=block2_early[:], func=ACT.Copy)

        scores = []
        for h in range(2):
            key_scales = sb.tile([P, HALF], U8, name=f"key_scales{h}", tag=f"key_scales{h}", align_bytes=64)
            entries = idx[:, h * HALF // LIST_ROWS : (h + 1) * HALF // LIST_ROWS]
            nc.vector.tensor_copy(key_scales[:], pool_scales[:].indirect(entries))
            scores.append(ps.tile([P, HALF], F32, name=f"scores{h}", tag=f"bank{h}"))
            nc.tensor.matmul_mx(
                out=scores[h][:], lhsT=q_codes[:].bitcast(FP8X4), lhsT_scale=q_scales[:],
                rhs=key_words[:, h * HALF : (h + 1) * HALF].bitcast(FP4X4), rhs_scale=key_scales[:],
                start=True, stop=True,
            )

        neg_half_a = sb.tile([P, I], F32, name="neg_half_a")
        neg_half_max = None
        for h in range(2):
            running = sb.tile([P, 1], F32, name=f"running{h}", tag=f"running{h}", align_bytes=64)
            nc.vector.tensor_scalar(
                out=neg_half_a[:, h * HALF : (h + 1) * HALF], in0=scores[h][:], scalar1=-0.5, scalar2=neg_half_max,
                op0=ALU.mult, op1=ALU.min, accum_out=running[:],
            )
            neg_half_max = running[:]
        neg_max = sb.tile([P, 1], F32, name="neg_max")
        nc.scalar.activation(out=neg_max[:], in_=neg_half_max, func=ACT.Copy, scale=2.0)
        nc.scalar.activation(out=pb[:, :I], in_=neg_half_a[:], func=ACT.Exp, scale=-1.0, bias=neg_half_max)
        pa = sb.tile([P, I], F32, name="pa")
        nc.scalar.activation(out=pa[:], in_=neg_half_a[:], func=ACT.Exp, scale=-2.0, bias=neg_max[:])

        factor_rows = ps.tile([P, PACK, P], F32, name="factor_rows", tag="bank2")
        for t in range(PACK):
            nc.tensor.transpose(factor_rows[:, t, :], factor_columns[:, t : t + 1].to_broadcast([P, P]), ident[:])

        v3_grouped = sb.tile([P, I], BF16, name="v3_grouped", tag="result2", align_bytes=64)
        v3_codes = sb.tile([P, P], U32, name="v3_codes", align_bytes=64)
        v3_scales = sb.tile([P, P], U8, name="v3_scales", align_bytes=64)

        v0_grouped = sb.tile([P, I], BF16, name="v0_grouped", align_bytes=64)
        turn(gather_vals(0), v0_grouped[:])

        p = sb.tile([P, I], F32, name="p", tag="vals0", align_bytes=64)
        nc.vector.tensor_tensor(p[:], pb[:].indirect(idx2[:]), pa[:], ALU.mult)

        p_summed = sb.tile([P, I], F32, name="p_summed")
        z = sb.tile([P, 1], F32, name="z")
        nc.scalar.activation(out=p_summed[:], in_=p[:], func=ACT.Copy, accum_out=z[:])
        nc.scalar.activation(out=block2_bf16[:, EARLY_TOKENS:], in_=block2_late[:], func=ACT.Copy)
        picked2 = sb.tile([P, I], BF16, name="picked2", align_bytes=64)
        nc.scalar.activation(out=picked2[:], in_=block2_bf16[:].indirect(idx[:]), func=ACT.Copy)

        picked1 = gather_vals(1)
        inv_z = sb.tile([P, 1], F32, name="inv_z", tag="vals1", align_bytes=64)
        nc.vector.reciprocal(out=inv_z[:], in_=z[:])
        wo = sb.tile([P, I], BF16, name="wo", align_bytes=64)
        nc.vector.scalar_tensor_tensor(
            out=wo[:].rearrange("q (s t) -> q s t", t=PACK),
            in0=p_summed[:].rearrange("q (s t) -> q s t", t=PACK),
            scalar=inv_z[:],
            in1=factor_rows[:].rearrange("q t s -> q s t"),
            op0=ALU.mult, op1=ALU.mult,
        )

        middle_grouped = sb.tile([P, 3 * I], BF16, name="middle_grouped", tag="block2_bf16", align_bytes=64)
        v1_grouped, v2_grouped, w_grouped = (middle_grouped[:, n * I : (n + 1) * I] for n in range(3))
        turn(picked1, v1_grouped)
        turn(wo, w_grouped)
        turn(picked2, v2_grouped)

        turn(gather_vals(3), v3_grouped[:])
        codes = sb.tile([P, 4 * P], U32, name="codes", tag="vals3", align_bytes=64)
        scales = sb.tile([P, 4 * P], U8, name="scales", align_bytes=64)
        for place, grouped in ((0, v0_grouped[:]), (1, v1_grouped), (3, w_grouped), (2, v2_grouped)):
            cols = slice(place * P, (place + 1) * P)
            quantise(codes[:, cols], scales[:, cols], grouped)
        quantise(v3_codes[:], v3_scales[:], v3_grouped[:])

        def product(first, last, v_codes, v_scales, bank, copy_out, queue):
            width = (last - first) * P
            acc = ps.tile([P, width], F32, name=f"acc{first}", tag=bank)
            nc.tensor.matmul_mx(
                out=acc[:], lhsT=codes[:, 3 * P :].bitcast(FP8X4), lhsT_scale=scales[:, 3 * P :],
                rhs=v_codes.bitcast(FP8X4), rhs_scale=v_scales, start=True, stop=True,
            )
            result = sb.tile([P, width], F32, name=f"result{first}", tag=f"result{first}", align_bytes=64)
            copy_out(out=result[:], in_=acc[:])
            queue.dma_start(out=out[:, first * P : last * P], in_=result[:])

        product(0, 2, codes[:, : 2 * P], scales[:, : 2 * P], "bank0", nc.scalar.copy, nc.sync)
        product(2, 3, codes[:, 2 * P : 3 * P], scales[:, 2 * P : 3 * P], "bank2", nc.vector.tensor_copy, nc.sync)
        product(3, 4, v3_codes[:], v3_scales[:], "bank1", nc.scalar.copy, nc.scalar)
